import numpy as np
import ml_dtypes


def mxq(x, axis, fmt="e4m3"):
    dtype, down = {"e4m3": (ml_dtypes.float8_e4m3fn, 7), "e5m2": (ml_dtypes.float8_e5m2, 14)}[fmt]
    v = np.moveaxis(np.asarray(x, np.float32).astype(ml_dtypes.bfloat16).astype(np.float64), axis, -1)
    blocks = v.reshape(v.shape[:-1] + (-1, 32))
    amax = np.abs(blocks).max(-1, keepdims=True)
    byte = np.maximum(np.where(amax > 0, np.frexp(amax)[1] - 1 + 127, 0) - down, 1)
    scale = np.exp2(byte - 127.0)
    codes = (blocks / scale).astype(np.float32).astype(dtype).astype(np.float64)
    return np.moveaxis((codes * scale).reshape(v.shape), -1, axis)


WIDE = False


def mx_kscale(k):
    if not WIDE:
        return np.ones(k)
    levels = np.array([10, -10, 5, -5, 0])
    if k % 512:
        return np.exp2(np.random.permutation(np.resize(levels, k // 32))).repeat(32)
    a = np.empty((k // 512, 16))
    for p in range(k // 512):
        a[p, :8] = np.random.permutation(np.resize(levels, 8))
        for g in range(8):
            far = levels[np.abs(levels - a[p, g]) >= 10]
            a[p, g + 8] = far[np.random.randint(len(far))]
    return np.exp2(a.ravel()).repeat(32)


def f64(x):
    return np.asarray(x).astype(np.float64)


def striped(idx):
    return np.tile(idx.reshape(-1, 16).T, (8, 1)).astype(np.uint16)


def unstriped(offs):
    return offs[:16].T.reshape(-1).astype(np.int64)


def gelu(v):
    return 0.5 * v * (1.0 + np.tanh(np.sqrt(2.0 / np.pi) * (v + 0.044715 * v**3)))


K, T, S, V, H, N, J = 512, 2048, 1024, 512, 512, 256, 512


def setup_inputs():
    n = np.random.standard_normal
    s = mx_kscale(K)[:, None]
    u = mx_kscale(H)
    r = mx_kscale(J)[:, None]
    return {
        "xT": (n((K, T)) * s).astype(np.float32),
        "eT": (n((J, V)) * r).astype(np.float32),
        "w1": (n((K, H)) / np.sqrt(3 * K) / s * u).astype(np.float32),
        "w2": (n((K, H)) / np.sqrt(3 * K) / s * u).astype(np.float32),
        "w3": (n((J, H)) / np.sqrt(3 * J) / r * u).astype(np.float32),
        "w4": (n((H, N)) / np.sqrt(H) / u[:, None]).astype(np.float32),
        "offs": striped(np.random.permutation(T)[:S]),
    }


def reference(xT, eT, w1, w2, w3, w4, offs):
    xq = mxq(f64(xT)[:, unstriped(offs)], 0, "e4m3")
    h = gelu(mxq(f64(w1), 0, "e4m3").T @ xq[:, :V] + mxq(f64(w2), 0, "e4m3").T @ xq[:, V:2 * V] + mxq(f64(w3), 0, "e4m3").T @ mxq(f64(eT), 0, "e4m3"))
    return mxq(f64(w4), 0, "e4m3").T @ mxq(h, 0, "e4m3")

@@ -1,0 +1,175 @@
+from contextlib import ExitStack
+
+import concourse.mybir as mybir
+
+K, T, S, V, H, N = 512, 2048, 1024, 512, 512, 256
+FLOPS = 2 * (3 * K * H * V + H * N * V)
+
+F32 = mybir.dt.float32
+BF16 = mybir.dt.bfloat16
+I32 = mybir.dt.int32
+U32 = mybir.dt.uint32
+U16 = mybir.dt.uint16
+U8 = mybir.dt.uint8
+FP8X4 = mybir.dt.float8_e4m3fn_x4
+COPY = mybir.ActivationFunctionType.Copy
+GELU = mybir.ActivationFunctionType.Gelu_apprx_tanh
+
+P = 128
+PACK = 4
+X_CHUNKS = (512, 512, 512, 256, 256)
+X_SCALAR_EIGHTHS = 3
+E_CHUNK = 128
+
+
+def cast(nc, on_scalar, dst, src):
+    if on_scalar:
+        nc.scalar.activation(dst, src, COPY)
+    else:
+        nc.vector.tensor_copy(dst, src)
+
+
+def weave(nc, on_scalar, grouped, raw, lo, hi):
+    cast(
+        nc,
+        on_scalar,
+        grouped[:, lo:hi, :].rearrange("p (c i) j -> p c j i", i=4),
+        raw[:, :, lo:hi].rearrange("p j (c i) -> p c j i", i=4),
+    )
+
+
+def weave_dealt(nc, on_scalar, grouped, raw):
+    cast(nc, on_scalar, grouped.rearrange("p t m j -> p m j t"), raw.rearrange("p j (m t) -> p m j t", t=PACK))
+
+
+def quantize(nc, codes, scales, grouped):
+    nc.vector.quantize_mx(out=codes.bitcast(FP8X4), scales=scales, in_=grouped)
+
+
+def tile_picked_edgeup_gelu_e_kernel(tc, xT, eT, w1, w2, w3, w4, offs, out):
+    nc = tc.nc
+    x_starts = [sum(X_CHUNKS[:g]) for g in range(len(X_CHUNKS))]
+    e_chunks = V // E_CHUNK
+
+    with ExitStack() as ctx:
+        sb = ctx.enter_context(tc.tile_pool(name="sb", bufs=1))
+        ps = ctx.enter_context(tc.psum_pool(name="ps", bufs=1))
+
+        def load(name, rows):
+            raw = sb.tile([P, PACK, rows.shape[1]], F32, name=name, align_bytes=64)
+            nc.sync.dma_start(out=raw[:], in_=rows.rearrange("(p j) w -> p j w", j=PACK))
+            return raw
+
+        def mx_tiles(name, width):
+            codes = sb.tile([P, width], U32, name=name + "_codes", align_bytes=64)
+            scales = sb.tile([P, width], U8, name=name + "_scales", align_bytes=64)
+            return codes, scales
+
+        x_raw = [load("x_raw%d" % g, xT[:, lo : lo + width]) for g, (lo, width) in enumerate(zip(x_starts, X_CHUNKS))]
+        offsets = sb.tile([P, S // 16], U16, name="offsets")
+        nc.sync.dma_start(offsets[:], offs)
+        w_raw = [load("w_raw%d" % a, w) for a, w in enumerate((w1, w2))]
+        w3_raw = [load("w3_raw%d" % b, w3[:, b * (H // 2) : (b + 1) * (H // 2)]) for b in range(2)]
+        e_raw = [load("e_raw%d" % c, eT[:, c * E_CHUNK : (c + 1) * E_CHUNK]) for c in range(e_chunks)]
+        w4_raw = load("w4_raw", w4)
+
+        zero = sb.tile([P, 1], F32, name="zero")
+        no_bias = sb.tile([P, 1], F32, name="no_bias")
+        nc.vector.memset(zero[:], 0.0)
+        nc.scalar.activation(no_bias[:], zero[:], GELU)
+
+        x_codes, x_scales = mx_tiles("x", T)
+        nc.vector.memset(x_scales[:].bitcast(I32), 0)
+        for g, (lo, width) in enumerate(zip(x_starts, X_CHUNKS)):
+            cols = slice(lo, lo + width)
+            cut = width * X_SCALAR_EIGHTHS // 8
+            x_bf = sb.tile([P, width, PACK], BF16, name="x_bf%d" % g, align_bytes=64)
+            weave(nc, True, x_bf, x_raw[g], 0, cut)
+            weave(nc, False, x_bf, x_raw[g], cut, width)
+            quantize(nc, x_codes[:, cols], x_scales[:, cols], x_bf[:].rearrange("p c j -> p (c j)"))
+
+        h_ps = [ps.tile([P, PACK, E_CHUNK], F32, name="h_ps%d" % c) for c in range(e_chunks)]
+        w_bf = [sb.tile([P, PACK, P, PACK], BF16, name="w_bf%d" % a, align_bytes=64) for a in range(3)]
+        w_mx = [mx_tiles("w%d" % a, H) for a in range(3)]
+
+        def first_layer_passes(a, c, codes, scales):
+            for t in range(PACK):
+                m = slice(t * P, (t + 1) * P)
+                nc.tensor.matmul_mx(
+                    out=h_ps[c][:, t, :],
+                    lhsT=w_mx[a][0][:, m].bitcast(FP8X4),
+                    lhsT_scale=w_mx[a][1][:, m],
+                    rhs=codes.bitcast(FP8X4),
+                    rhs_scale=scales,
+                    start=(a == 0 and t == 0),
+                    stop=(a == 2 and t == PACK - 1),
+                )
+
+        def quantize_w(a, parts):
+            flat = w_bf[a][:].rearrange("p t m j -> p (t m j)")
+            width = H // parts
+            for b in range(parts):
+                cols = slice(b * width, (b + 1) * width)
+                quantize(nc, w_mx[a][0][:, cols], w_mx[a][1][:, cols], flat[:, PACK * b * width : PACK * (b + 1) * width])
+
+        ends = []
+        for a in range(2):
+            piece = offsets[:, a * (V // 16) : (a + 1) * (V // 16)]
+            end_codes = sb.tile([P, V], U32, name="end_codes%d" % a, align_bytes=64)
+            nc.vector.tensor_copy(end_codes[:], x_codes[:].indirect(piece))
+            if a == 1:
+                weave_dealt(nc, True, w_bf[0][:], w_raw[0][:])
+                quantize_w(0, 1)
+            end_scales = sb.tile([P, V], U8, name="end_scales%d" % a, tag=("w_bf0" if a == 1 else "end_scales0"), align_bytes=64)
+            nc.vector.tensor_copy(end_scales[:], x_scales[:].indirect(piece))
+            ends.append((end_codes, end_scales))
+
+        def end_passes(a, c):
+            cols = slice(c * E_CHUNK, (c + 1) * E_CHUNK)
+            first_layer_passes(a, c, ends[a][0][:, cols], ends[a][1][:, cols])
+
+        for c in range(e_chunks):
+            end_passes(0, c)
+        weave_dealt(nc, True, w_bf[1][:], w_raw[1][:])
+        quantize_w(1, 1)
+        weave_dealt(nc, True, w_bf[2][:, :, 0 : P // 2, :], w3_raw[0][:])
+        weave_dealt(nc, False, w_bf[2][:, :, P // 2 : P, :], w3_raw[1][:])
+        quantize_w(2, 2)
+
+        h_bf = []
+        for c in range(e_chunks):
+            e_bf = sb.tile([P, E_CHUNK, PACK], BF16, name="e_bf%d" % c, align_bytes=64)
+            weave(nc, c < 2, e_bf, e_raw[c], 0, E_CHUNK)
+            e_codes, e_scales = mx_tiles("e%d" % c, E_CHUNK)
+            quantize(nc, e_codes[:], e_scales[:], e_bf[:].rearrange("p c j -> p (c j)"))
+            end_passes(1, c)
+            first_layer_passes(2, c, e_codes[:], e_scales[:])
+        for c in range(e_chunks):
+            hb = sb.tile([P, E_CHUNK, PACK], BF16, name="h_bf%d" % c, align_bytes=64)
+            nc.scalar.activation(hb[:], h_ps[c][:].rearrange("p t n -> p n t"), GELU, bias=no_bias[:])
+            h_bf.append(hb)
+
+        w4_bf = sb.tile([P, N, PACK], BF16, name="w4_bf", align_bytes=64)
+        weave(nc, False, w4_bf, w4_raw, 0, N)
+        w4_codes, w4_scales = mx_tiles("w4", N)
+        quantize(nc, w4_codes[:], w4_scales[:], w4_bf[:].rearrange("p c j -> p (c j)"))
+
+        out_rows = out.rearrange("(a p) n -> p a n", p=P)
+        for c in range(e_chunks):
+            h_codes, h_scales = mx_tiles("h%d" % c, E_CHUNK)
+            quantize(nc, h_codes[:], h_scales[:], h_bf[c][:].rearrange("p n t -> p (n t)"))
+            o_ps = ps.tile([P, N // P, E_CHUNK], F32, name="o_ps%d" % c)
+            for a in range(N // P):
+                m = slice(a * P, (a + 1) * P)
+                nc.tensor.matmul_mx(
+                    out=o_ps[:, a, :],
+                    lhsT=w4_codes[:, m].bitcast(FP8X4),
+                    lhsT_scale=w4_scales[:, m],
+                    rhs=h_codes[:].bitcast(FP8X4),
+                    rhs_scale=h_scales[:],
+                    start=True,
+                    stop=True,
+                )
+            o_sb = sb.tile([P, N // P, E_CHUNK], F32, name="o_sb%d" % c, align_bytes=64)
+            cast(nc, c != 2, o_sb[:], o_ps[:])
+            nc.sync.dma_start(out=out_rows[:, :, c * E_CHUNK : (c + 1) * E_CHUNK], in_=o_sb[:])

@@ -18,7 +18,7 @@ GELU = mybir.ActivationFunctionType.Gelu_apprx_tanh
 P = 128
 PACK = 4
 X_CHUNKS = (512, 512, 512, 256, 256)
-X_SCALAR_EIGHTHS = 3
+X_PIECES = ((0, 0, 512, True), (1, 0, 512, False), (2, 0, 256, True), (2, 256, 256, False), (3, 0, 256, True), (4, 0, 128, False), (4, 128, 128, True))
 E_CHUNK = 128
 
 
@@ -29,13 +29,8 @@ def cast(nc, on_scalar, dst, src):
         nc.vector.tensor_copy(dst, src)
 
 
-def weave(nc, on_scalar, grouped, raw, lo, hi):
-    cast(
-        nc,
-        on_scalar,
-        grouped[:, lo:hi, :].rearrange("p (c i) j -> p c j i", i=4),
-        raw[:, :, lo:hi].rearrange("p j (c i) -> p c j i", i=4),
-    )
+def weave(nc, on_scalar, grouped, raw):
+    cast(nc, on_scalar, grouped.rearrange("p (c i) j -> p c j i", i=4), raw.rearrange("p j (c i) -> p c j i", i=4))
 
 
 def weave_dealt(nc, on_scalar, grouped, raw):
@@ -68,9 +63,8 @@ def tile_picked_edgeup_gelu_e_kernel(tc, xT, eT, w1, w2, w3, w4, offs, out):
         x_raw = [load("x_raw%d" % g, xT[:, lo : lo + width]) for g, (lo, width) in enumerate(zip(x_starts, X_CHUNKS))]
         offsets = sb.tile([P, S // 16], U16, name="offsets")
         nc.sync.dma_start(offsets[:], offs)
-        w_raw = [load("w_raw%d" % a, w) for a, w in enumerate((w1, w2))]
-        w3_raw = [load("w3_raw%d" % b, w3[:, b * (H // 2) : (b + 1) * (H // 2)]) for b in range(2)]
-        e_raw = [load("e_raw%d" % c, eT[:, c * E_CHUNK : (c + 1) * E_CHUNK]) for c in range(e_chunks)]
+        w_raw = [load("w_raw%d" % a, w) for a, w in enumerate((w1, w2, w3))]
+        e_raw = [load("e_raw%d" % b, eT[:, b * (V // 2) : (b + 1) * (V // 2)]) for b in range(2)]
         w4_raw = load("w4_raw", w4)
 
         zero = sb.tile([P, 1], F32, name="zero")
@@ -80,16 +74,14 @@ def tile_picked_edgeup_gelu_e_kernel(tc, xT, eT, w1, w2, w3, w4, offs, out):
 
         x_codes, x_scales = mx_tiles("x", T)
         nc.vector.memset(x_scales[:].bitcast(I32), 0)
-        for g, (lo, width) in enumerate(zip(x_starts, X_CHUNKS)):
-            cols = slice(lo, lo + width)
-            cut = width * X_SCALAR_EIGHTHS // 8
-            x_bf = sb.tile([P, width, PACK], BF16, name="x_bf%d" % g, align_bytes=64)
-            weave(nc, True, x_bf, x_raw[g], 0, cut)
-            weave(nc, False, x_bf, x_raw[g], cut, width)
+        for n, (g, lo, width, on_scalar) in enumerate(X_PIECES):
+            cols = slice(x_starts[g] + lo, x_starts[g] + lo + width)
+            x_bf = sb.tile([P, width, PACK], BF16, name="x_bf%d" % n, align_bytes=64)
+            weave(nc, on_scalar, x_bf[:], x_raw[g][:, :, lo : lo + width])
             quantize(nc, x_codes[:, cols], x_scales[:, cols], x_bf[:].rearrange("p c j -> p (c j)"))
 
         h_ps = [ps.tile([P, PACK, E_CHUNK], F32, name="h_ps%d" % c) for c in range(e_chunks)]
-        w_bf = [sb.tile([P, PACK, P, PACK], BF16, name="w_bf%d" % a, align_bytes=64) for a in range(3)]
+        w_bf = [sb.tile([P, PACK, P, PACK], BF16, name="w_bf%d" % a, align_bytes=64) for a in range(2)]
         w_mx = [mx_tiles("w%d" % a, H) for a in range(3)]
 
         def first_layer_passes(a, c, codes, scales):
@@ -105,12 +97,9 @@ def tile_picked_edgeup_gelu_e_kernel(tc, xT, eT, w1, w2, w3, w4, offs, out):
                     stop=(a == 2 and t == PACK - 1),
                 )
 
-        def quantize_w(a, parts):
-            flat = w_bf[a][:].rearrange("p t m j -> p (t m j)")
-            width = H // parts
-            for b in range(parts):
-                cols = slice(b * width, (b + 1) * width)
-                quantize(nc, w_mx[a][0][:, cols], w_mx[a][1][:, cols], flat[:, PACK * b * width : PACK * (b + 1) * width])
+        def prepare_w(a):
+            weave_dealt(nc, True, w_bf[a][:], w_raw[a][:])
+            quantize(nc, w_mx[a][0][:], w_mx[a][1][:], w_bf[a][:].rearrange("p t m j -> p (t m j)"))
 
         ends = []
         for a in range(2):
@@ -118,8 +107,7 @@ def tile_picked_edgeup_gelu_e_kernel(tc, xT, eT, w1, w2, w3, w4, offs, out):
             end_codes = sb.tile([P, V], U32, name="end_codes%d" % a, align_bytes=64)
             nc.vector.tensor_copy(end_codes[:], x_codes[:].indirect(piece))
             if a == 1:
-                weave_dealt(nc, True, w_bf[0][:], w_raw[0][:])
-                quantize_w(0, 1)
+                prepare_w(0)
             end_scales = sb.tile([P, V], U8, name="end_scales%d" % a, tag=("w_bf0" if a == 1 else "end_scales0"), align_bytes=64)
             nc.vector.tensor_copy(end_scales[:], x_scales[:].indirect(piece))
             ends.append((end_codes, end_scales))
@@ -130,35 +118,49 @@ def tile_picked_edgeup_gelu_e_kernel(tc, xT, eT, w1, w2, w3, w4, offs, out):
 
         for c in range(e_chunks):
             end_passes(0, c)
-        weave_dealt(nc, True, w_bf[1][:], w_raw[1][:])
-        quantize_w(1, 1)
-        weave_dealt(nc, True, w_bf[2][:, :, 0 : P // 2, :], w3_raw[0][:])
-        weave_dealt(nc, False, w_bf[2][:, :, P // 2 : P, :], w3_raw[1][:])
-        quantize_w(2, 2)
+        prepare_w(1)
+        w3_dealt = w_raw[2][:].rearrange("p j (m t) -> p m j t", t=PACK)
+        for b in (1, 0):
+            half = sb.tile([P, 2, P, PACK], BF16, name="w3_bf%d" % b, tag=("w_bf1" if b == 1 else "w3_bf0"), align_bytes=64)
+            cast(nc, b == 0, half[:].rearrange("p t m j -> p m j t"), w3_dealt[:, :, :, 2 * b : 2 * b + 2])
+            cols = slice(b * (H // 2), (b + 1) * (H // 2))
+            quantize(nc, w_mx[2][0][:, cols], w_mx[2][1][:, cols], half[:].rearrange("p t m j -> p (t m j)"))
 
-        h_bf = []
+        e_mx = []
         for c in range(e_chunks):
             e_bf = sb.tile([P, E_CHUNK, PACK], BF16, name="e_bf%d" % c, align_bytes=64)
-            weave(nc, c < 2, e_bf, e_raw[c], 0, E_CHUNK)
+            lo = (c % 2) * E_CHUNK
+            weave(nc, c < 3, e_bf[:], e_raw[c // 2][:, :, lo : lo + E_CHUNK])
             e_codes, e_scales = mx_tiles("e%d" % c, E_CHUNK)
             quantize(nc, e_codes[:], e_scales[:], e_bf[:].rearrange("p c j -> p (c j)"))
-            end_passes(1, c)
-            first_layer_passes(2, c, e_codes[:], e_scales[:])
+            e_mx.append((e_codes[:], e_scales[:]))
+
+        groups = ((0, 1), (2,), (3,))
+        h_bf = [sb.tile([P, len(g) * E_CHUNK, PACK], BF16, name="h_bf%d" % g[0], align_bytes=64) for g in groups]
         for c in range(e_chunks):
-            hb = sb.tile([P, E_CHUNK, PACK], BF16, name="h_bf%d" % c, align_bytes=64)
-            nc.scalar.activation(hb[:], h_ps[c][:].rearrange("p t n -> p n t"), GELU, bias=no_bias[:])
-            h_bf.append(hb)
+            end_passes(1, c)
+            first_layer_passes(2, c, e_mx[c][0], e_mx[c][1])
+        for g, chunks in enumerate(groups):
+            for c in chunks:
+                cols = slice((c - chunks[0]) * E_CHUNK, (c - chunks[0] + 1) * E_CHUNK)
+                nc.scalar.activation(h_bf[g][:, cols, :], h_ps[c][:].rearrange("p t n -> p n t"), GELU, bias=no_bias[:])
 
         w4_bf = sb.tile([P, N, PACK], BF16, name="w4_bf", align_bytes=64)
-        weave(nc, False, w4_bf, w4_raw, 0, N)
+        weave(nc, False, w4_bf[:], w4_raw[:])
         w4_codes, w4_scales = mx_tiles("w4", N)
-        quantize(nc, w4_codes[:], w4_scales[:], w4_bf[:].rearrange("p c j -> p (c j)"))
+        h_mx = []
+        for g, chunks in enumerate(groups):
+            h_codes, h_scales = mx_tiles("h%d" % g, len(chunks) * E_CHUNK)
+            quantize(nc, h_codes[:], h_scales[:], h_bf[g][:].rearrange("p n t -> p (n t)"))
+            h_mx.append((h_codes, h_scales))
+            if g == 0:
+                quantize(nc, w4_codes[:], w4_scales[:], w4_bf[:].rearrange("p c j -> p (c j)"))
 
         out_rows = out.rearrange("(a p) n -> p a n", p=P)
-        for c in range(e_chunks):
-            h_codes, h_scales = mx_tiles("h%d" % c, E_CHUNK)
-            quantize(nc, h_codes[:], h_scales[:], h_bf[c][:].rearrange("p n t -> p (n t)"))
-            o_ps = ps.tile([P, N // P, E_CHUNK], F32, name="o_ps%d" % c)
+        for g, chunks in enumerate(groups):
+            width = len(chunks) * E_CHUNK
+            h_codes, h_scales = h_mx[g]
+            o_ps = ps.tile([P, N // P, width], F32, name="o_ps%d" % g)
             for a in range(N // P):
                 m = slice(a * P, (a + 1) * P)
                 nc.tensor.matmul_mx(
@@ -170,6 +172,7 @@ def tile_picked_edgeup_gelu_e_kernel(tc, xT, eT, w1, w2, w3, w4, offs, out):
                     start=True,
                     stop=True,
                 )
-            o_sb = sb.tile([P, N // P, E_CHUNK], F32, name="o_sb%d" % c, align_bytes=64)
-            cast(nc, c != 2, o_sb[:], o_ps[:])
-            nc.sync.dma_start(out=out_rows[:, :, c * E_CHUNK : (c + 1) * E_CHUNK], in_=o_sb[:])
+            o_sb = sb.tile([P, N // P, width], F32, name="o_sb%d" % g, align_bytes=64)
+            cast(nc, g == 0, o_sb[:], o_ps[:])
+            lo = chunks[0] * E_CHUNK
+            nc.sync.dma_start(out=out_rows[:, :, lo : lo + width], in_=o_sb[:])

@@ -17,8 +17,6 @@ GELU = mybir.ActivationFunctionType.Gelu_apprx_tanh
 
 P = 128
 PACK = 4
-X_CHUNKS = (512, 512, 512, 256, 256)
-X_PIECES = ((0, 0, 512, True), (1, 0, 512, False), (2, 0, 256, True), (2, 256, 256, False), (3, 0, 256, True), (4, 0, 128, False), (4, 128, 128, True))
 E_CHUNK = 128
 
 
@@ -41,9 +39,12 @@ def quantize(nc, codes, scales, grouped):
     nc.vector.quantize_mx(out=codes.bitcast(FP8X4), scales=scales, in_=grouped)
 
 
+def weave_pair(nc, on_scalar, grouped, u, picked):
+    cast(nc, on_scalar, grouped.rearrange("p (c i) j -> p c j i", i=4)[:, :, 2 * u : 2 * u + 2, :], picked.rearrange("p j (c i) -> p c j i", i=4))
+
+
 def tile_picked_edgeup_gelu_e_kernel(tc, xT, eT, w1, w2, w3, w4, offs, out):
     nc = tc.nc
-    x_starts = [sum(X_CHUNKS[:g]) for g in range(len(X_CHUNKS))]
     e_chunks = V // E_CHUNK
 
     with ExitStack() as ctx:
@@ -60,9 +61,15 @@ def tile_picked_edgeup_gelu_e_kernel(tc, xT, eT, w1, w2, w3, w4, offs, out):
             scales = sb.tile([P, width], U8, name=name + "_scales", align_bytes=64)
             return codes, scales
 
-        x_raw = [load("x_raw%d" % g, xT[:, lo : lo + width]) for g, (lo, width) in enumerate(zip(x_starts, X_CHUNKS))]
+        x_rows = xT.rearrange("(p j) t -> p j t", j=PACK)
         offsets = sb.tile([P, S // 16], U16, name="offsets")
-        nc.sync.dma_start(offsets[:], offs)
+        x_planes = []
+        for j in range(PACK):
+            plane = sb.tile([P, T], F32, name="x_plane%d" % j, align_bytes=64)
+            nc.sync.dma_start(out=plane[:], in_=x_rows[:, j, :])
+            x_planes.append(plane)
+            if j == 0:
+                nc.sync.dma_start(offsets[:], offs)
         w_raw = [load("w_raw%d" % a, w) for a, w in enumerate((w1, w2, w3))]
         e_raw = [load("e_raw%d" % b, eT[:, b * (V // 2) : (b + 1) * (V // 2)]) for b in range(2)]
         w4_raw = load("w4_raw", w4)
@@ -72,16 +79,25 @@ def tile_picked_edgeup_gelu_e_kernel(tc, xT, eT, w1, w2, w3, w4, offs, out):
         nc.vector.memset(zero[:], 0.0)
         nc.scalar.activation(no_bias[:], zero[:], GELU)
 
-        x_codes, x_scales = mx_tiles("x", T)
-        nc.vector.memset(x_scales[:].bitcast(I32), 0)
-        for n, (g, lo, width, on_scalar) in enumerate(X_PIECES):
-            cols = slice(x_starts[g] + lo, x_starts[g] + lo + width)
-            x_bf = sb.tile([P, width, PACK], BF16, name="x_bf%d" % n, align_bytes=64)
-            weave(nc, on_scalar, x_bf[:], x_raw[g][:, :, lo : lo + width])
-            quantize(nc, x_codes[:, cols], x_scales[:, cols], x_bf[:].rearrange("p c j -> p (c j)"))
+        end_bf = [sb.tile([P, V, PACK], BF16, name="end_bf%d" % a, align_bytes=64) for a in range(2)]
+        first_pair = sb.tile([P, 2, S], F32, name="first_pair", align_bytes=64)
+        for j in range(2):
+            nc.vector.tensor_copy(first_pair[:, j, :], x_planes[j][:].indirect(offsets[:]))
+        for a in range(2):
+            weave_pair(nc, True, end_bf[a][:], 0, first_pair[:, :, a * V : (a + 1) * V])
+        second_pair = [sb.tile([P, 2, V], F32, name="second_pair%d" % a, align_bytes=64) for a in range(2)]
+        for j in range(2):
+            for a in range(2):
+                piece = offsets[:, a * (V // 16) : (a + 1) * (V // 16)]
+                nc.vector.tensor_copy(second_pair[a][:, j, :], x_planes[2 + j][:].indirect(piece))
+        for a in range(2):
+            weave_pair(nc, False, end_bf[a][:], 1, second_pair[a][:])
+        ends = [mx_tiles("end%d" % a, V) for a in range(2)]
+
+        def quantize_end(a):
+            quantize(nc, ends[a][0][:], ends[a][1][:], end_bf[a][:].rearrange("p c j -> p (c j)"))
 
         h_ps = [ps.tile([P, PACK, E_CHUNK], F32, name="h_ps%d" % c) for c in range(e_chunks)]
-        w_bf = [sb.tile([P, PACK, P, PACK], BF16, name="w_bf%d" % a, align_bytes=64) for a in range(2)]
         w_mx = [mx_tiles("w%d" % a, H) for a in range(3)]
 
         def first_layer_passes(a, c, codes, scales):
@@ -97,47 +113,42 @@ def tile_picked_edgeup_gelu_e_kernel(tc, xT, eT, w1, w2, w3, w4, offs, out):
                     stop=(a == 2 and t == PACK - 1),
                 )
 
-        def prepare_w(a):
-            weave_dealt(nc, True, w_bf[a][:], w_raw[a][:])
-            quantize(nc, w_mx[a][0][:], w_mx[a][1][:], w_bf[a][:].rearrange("p t m j -> p (t m j)"))
+        def cast_w(a, lo, tiles, on_scalar):
+            dealt = w_raw[a][:].rearrange("p j (m t) -> p m j t", t=PACK)
+            part = sb.tile([P, tiles, P, PACK], BF16, name="w%d_bf%d" % (a, lo), align_bytes=64)
+            cast(nc, on_scalar, part[:].rearrange("p t m j -> p m j t"), dealt[:, :, :, lo : lo + tiles])
+            return part
 
-        ends = []
+        def quantize_w(a, lo, tiles, part):
+            cols = slice(lo * P, (lo + tiles) * P)
+            quantize(nc, w_mx[a][0][:, cols], w_mx[a][1][:, cols], part[:].rearrange("p t m j -> p (t m j)"))
+
         for a in range(2):
-            piece = offsets[:, a * (V // 16) : (a + 1) * (V // 16)]
-            end_codes = sb.tile([P, V], U32, name="end_codes%d" % a, align_bytes=64)
-            nc.vector.tensor_copy(end_codes[:], x_codes[:].indirect(piece))
-            if a == 1:
-                prepare_w(0)
-            end_scales = sb.tile([P, V], U8, name="end_scales%d" % a, tag=("w_bf0" if a == 1 else "end_scales0"), align_bytes=64)
-            nc.vector.tensor_copy(end_scales[:], x_scales[:].indirect(piece))
-            ends.append((end_codes, end_scales))
-
-        def end_passes(a, c):
-            cols = slice(c * E_CHUNK, (c + 1) * E_CHUNK)
-            first_layer_passes(a, c, ends[a][0][:, cols], ends[a][1][:, cols])
-
-        for c in range(e_chunks):
-            end_passes(0, c)
-        prepare_w(1)
-        w3_dealt = w_raw[2][:].rearrange("p j (m t) -> p m j t", t=PACK)
-        for b in (1, 0):
-            half = sb.tile([P, 2, P, PACK], BF16, name="w3_bf%d" % b, tag=("w_bf1" if b == 1 else "w3_bf0"), align_bytes=64)
-            cast(nc, b == 0, half[:].rearrange("p t m j -> p m j t"), w3_dealt[:, :, :, 2 * b : 2 * b + 2])
-            cols = slice(b * (H // 2), (b + 1) * (H // 2))
-            quantize(nc, w_mx[2][0][:, cols], w_mx[2][1][:, cols], half[:].rearrange("p t m j -> p (t m j)"))
+            halves = [cast_w(a, lo, 2, True) for lo in (0, 2)]
+            quantize_end(a)
+            for lo in (0, 2):
+                quantize_w(a, lo, 2, halves[lo // 2])
+        halves = [cast_w(2, lo, 2, lo == 2) for lo in (0, 2)]
+        for lo in (0, 2):
+            quantize_w(2, lo, 2, halves[lo // 2])
 
         e_mx = []
         for c in range(e_chunks):
             e_bf = sb.tile([P, E_CHUNK, PACK], BF16, name="e_bf%d" % c, align_bytes=64)
             lo = (c % 2) * E_CHUNK
-            weave(nc, c < 3, e_bf[:], e_raw[c // 2][:, :, lo : lo + E_CHUNK])
+            weave(nc, c < 2, e_bf[:], e_raw[c // 2][:, :, lo : lo + E_CHUNK])
             e_codes, e_scales = mx_tiles("e%d" % c, E_CHUNK)
             quantize(nc, e_codes[:], e_scales[:], e_bf[:].rearrange("p c j -> p (c j)"))
             e_mx.append((e_codes[:], e_scales[:]))
 
+        def end_passes(a, c):
+            cols = slice(c * E_CHUNK, (c + 1) * E_CHUNK)
+            first_layer_passes(a, c, ends[a][0][:, cols], ends[a][1][:, cols])
+
         groups = ((0, 1), (2,), (3,))
         h_bf = [sb.tile([P, len(g) * E_CHUNK, PACK], BF16, name="h_bf%d" % g[0], align_bytes=64) for g in groups]
         for c in range(e_chunks):
+            end_passes(0, c)
             end_passes(1, c)
             first_layer_passes(2, c, e_mx[c][0], e_mx[c][1])
         for g, chunks in enumerate(groups):

@@ -92,16 +92,19 @@ def tile_picked_edgeup_gelu_e_kernel(tc, xT, eT, w1, w2, w3, w4, offs, out):
                 nc.vector.tensor_copy(second_pair[a][:, j, :], x_planes[2 + j][:].indirect(piece))
         for a in range(2):
             weave_pair(nc, False, end_bf[a][:], 1, second_pair[a][:])
-        ends = [mx_tiles("end%d" % a, V) for a in range(2)]
+        ends = []
 
-        def quantize_end(a):
-            quantize(nc, ends[a][0][:], ends[a][1][:], end_bf[a][:].rearrange("p c j -> p (c j)"))
+        def quantize_end(a, scales_tag):
+            codes = sb.tile([P, V], U32, name="end%d_codes" % a, align_bytes=64)
+            scales = sb.tile([P, V], U8, name="end%d_scales" % a, tag=scales_tag, align_bytes=64)
+            quantize(nc, codes[:], scales[:], end_bf[a][:].rearrange("p c j -> p (c j)"))
+            ends.append((codes, scales))
 
         h_ps = [ps.tile([P, PACK, E_CHUNK], F32, name="h_ps%d" % c) for c in range(e_chunks)]
         w_mx = [mx_tiles("w%d" % a, H) for a in range(3)]
 
-        def first_layer_passes(a, c, codes, scales):
-            for t in range(PACK):
+        def first_layer_passes(a, c, codes, scales, tiles):
+            for t in tiles:
                 m = slice(t * P, (t + 1) * P)
                 nc.tensor.matmul_mx(
                     out=h_ps[c][:, t, :],
@@ -123,34 +126,37 @@ def tile_picked_edgeup_gelu_e_kernel(tc, xT, eT, w1, w2, w3, w4, offs, out):
             cols = slice(lo * P, (lo + tiles) * P)
             quantize(nc, w_mx[a][0][:, cols], w_mx[a][1][:, cols], part[:].rearrange("p t m j -> p (t m j)"))
 
-        for a in range(2):
-            halves = [cast_w(a, lo, 2, True) for lo in (0, 2)]
-            quantize_end(a)
+        halves = [cast_w(0, lo, 2, True) for lo in (0, 2)]
+        quantize_end(0, "end0_scales")
+        quantize_w(0, 0, 2, halves[0])
+        quantize_end(1, "w0_bf0")
+        quantize_w(0, 2, 2, halves[1])
+        for a in (1, 2):
+            halves = [cast_w(a, lo, 2, a == 1 or lo == 2) for lo in (0, 2)]
             for lo in (0, 2):
                 quantize_w(a, lo, 2, halves[lo // 2])
-        halves = [cast_w(2, lo, 2, lo == 2) for lo in (0, 2)]
-        for lo in (0, 2):
-            quantize_w(2, lo, 2, halves[lo // 2])
 
         e_mx = []
         for c in range(e_chunks):
             e_bf = sb.tile([P, E_CHUNK, PACK], BF16, name="e_bf%d" % c, align_bytes=64)
             lo = (c % 2) * E_CHUNK
-            weave(nc, c < 2, e_bf[:], e_raw[c // 2][:, :, lo : lo + E_CHUNK])
+            weave(nc, c < 3, e_bf[:], e_raw[c // 2][:, :, lo : lo + E_CHUNK])
             e_codes, e_scales = mx_tiles("e%d" % c, E_CHUNK)
             quantize(nc, e_codes[:], e_scales[:], e_bf[:].rearrange("p c j -> p (c j)"))
             e_mx.append((e_codes[:], e_scales[:]))
 
-        def end_passes(a, c):
+        def end_passes(a, c, tiles):
             cols = slice(c * E_CHUNK, (c + 1) * E_CHUNK)
-            first_layer_passes(a, c, ends[a][0][:, cols], ends[a][1][:, cols])
+            first_layer_passes(a, c, ends[a][0][:, cols], ends[a][1][:, cols], tiles)
 
         groups = ((0, 1), (2,), (3,))
         h_bf = [sb.tile([P, len(g) * E_CHUNK, PACK], BF16, name="h_bf%d" % g[0], align_bytes=64) for g in groups]
+        for a in range(2):
+            for tiles in ((0, 1), (2, 3)):
+                for c in range(e_chunks):
+                    end_passes(a, c, tiles)
         for c in range(e_chunks):
-            end_passes(0, c)
-            end_passes(1, c)
-            first_layer_passes(2, c, e_mx[c][0], e_mx[c][1])
+            first_layer_passes(2, c, e_mx[c][0], e_mx[c][1], range(PACK))
         for g, chunks in enumerate(groups):
             for c in chunks:
                 cols = slice((c - chunks[0]) * E_CHUNK, (c - chunks[0] + 1) * E_CHUNK)
@@ -168,12 +174,14 @@ def tile_picked_edgeup_gelu_e_kernel(tc, xT, eT, w1, w2, w3, w4, offs, out):
                 quantize(nc, w4_codes[:], w4_scales[:], w4_bf[:].rearrange("p c j -> p (c j)"))
 
         out_rows = out.rearrange("(a p) n -> p a n", p=P)
-        for g, chunks in enumerate(groups):
+        stores = ((0, 0, 1, True), (0, 1, 1, True), (1, 0, 2, False), (2, 0, 2, False))
+        for g, a0, blocks, on_scalar in stores:
+            chunks = groups[g]
             width = len(chunks) * E_CHUNK
             h_codes, h_scales = h_mx[g]
-            o_ps = ps.tile([P, N // P, width], F32, name="o_ps%d" % g)
-            for a in range(N // P):
-                m = slice(a * P, (a + 1) * P)
+            o_ps = ps.tile([P, blocks, width], F32, name="o_ps%d_%d" % (g, a0))
+            for a in range(blocks):
+                m = slice((a0 + a) * P, (a0 + a + 1) * P)
                 nc.tensor.matmul_mx(
                     out=o_ps[:, a, :],
                     lhsT=w4_codes[:, m].bitcast(FP8X4),
@@ -183,7 +191,7 @@ def tile_picked_edgeup_gelu_e_kernel(tc, xT, eT, w1, w2, w3, w4, offs, out):
                     start=True,
                     stop=True,
                 )
-            o_sb = sb.tile([P, N // P, width], F32, name="o_sb%d" % g, align_bytes=64)
-            cast(nc, g == 0, o_sb[:], o_ps[:])
+            o_sb = sb.tile([P, blocks, width], F32, name="o_sb%d_%d" % (g, a0), align_bytes=64)
+            cast(nc, on_scalar, o_sb[:], o_ps[:])
             lo = chunks[0] * E_CHUNK
-            nc.sync.dma_start(out=out_rows[:, :, lo : lo + width], in_=o_sb[:])
+            nc.sync.dma_start(out=out_rows[:, a0 : a0 + blocks, lo : lo + width], in_=o_sb[:])

@@ -80,9 +80,14 @@ def tile_picked_edgeup_gelu_e_kernel(tc, xT, eT, w1, w2, w3, w4, offs, out):
         nc.scalar.activation(no_bias[:], zero[:], GELU)
 
         end_bf = [sb.tile([P, V, PACK], BF16, name="end_bf%d" % a, align_bytes=64) for a in range(2)]
-        first_pair = sb.tile([P, 2, S], F32, name="first_pair", align_bytes=64)
-        for j in range(2):
-            nc.vector.tensor_copy(first_pair[:, j, :], x_planes[j][:].indirect(offsets[:]))
+        first_pair = sb.tile([P, 2, S], BF16, name="first_pair", align_bytes=64)
+        nc.vector.tensor_copy(first_pair[:, 0, :], x_planes[0][:].indirect(offsets[:]))
+        plane1_bf = sb.tile([P, T], BF16, name="plane1_bf", align_bytes=64)
+        for half in range(2):
+            cols = slice(half * (T // 2), (half + 1) * (T // 2))
+            cast(nc, half == 0, plane1_bf[:, cols], x_planes[1][:, cols])
+        nc.scalar.activation(first_pair[:, 1, 0:V], plane1_bf[:].indirect(offsets[:, 0 : V // 16]), COPY)
+        nc.vector.tensor_copy(first_pair[:, 1, V:S], x_planes[1][:].indirect(offsets[:, V // 16 : S // 16]))
         for a in range(2):
             weave_pair(nc, True, end_bf[a][:], 0, first_pair[:, :, a * V : (a + 1) * V])
         second_pair = [sb.tile([P, 2, V], F32, name="second_pair%d" % a, align_bytes=64) for a in range(2)]
@@ -140,7 +145,7 @@ def tile_picked_edgeup_gelu_e_kernel(tc, xT, eT, w1, w2, w3, w4, offs, out):
         for c in range(e_chunks):
             e_bf = sb.tile([P, E_CHUNK, PACK], BF16, name="e_bf%d" % c, align_bytes=64)
             lo = (c % 2) * E_CHUNK
-            weave(nc, c < 3, e_bf[:], e_raw[c // 2][:, :, lo : lo + E_CHUNK])
+            weave(nc, c < 2, e_bf[:], e_raw[c // 2][:, :, lo : lo + E_CHUNK])
             e_codes, e_scales = mx_tiles("e%d" % c, E_CHUNK)
             quantize(nc, e_codes[:], e_scales[:], e_bf[:].rearrange("p c j -> p (c j)"))
             e_mx.append((e_codes[:], e_scales[:]))

@@ -154,7 +154,7 @@ def tile_picked_edgeup_gelu_e_kernel(tc, xT, eT, w1, w2, w3, w4, offs, out):
             cols = slice(c * E_CHUNK, (c + 1) * E_CHUNK)
             first_layer_passes(a, c, ends[a][0][:, cols], ends[a][1][:, cols], tiles)
 
-        groups = ((0, 1), (2,), (3,))
+        groups = ((0, 1), (2, 3))
         h_bf = [sb.tile([P, len(g) * E_CHUNK, PACK], BF16, name="h_bf%d" % g[0], align_bytes=64) for g in groups]
         for a in range(2):
             for tiles in ((0, 1), (2, 3)):
@@ -173,13 +173,16 @@ def tile_picked_edgeup_gelu_e_kernel(tc, xT, eT, w1, w2, w3, w4, offs, out):
         h_mx = []
         for g, chunks in enumerate(groups):
             h_codes, h_scales = mx_tiles("h%d" % g, len(chunks) * E_CHUNK)
-            quantize(nc, h_codes[:], h_scales[:], h_bf[g][:].rearrange("p n t -> p (n t)"))
+            step = len(chunks) * E_CHUNK if g == 0 else E_CHUNK
+            for lo in range(0, len(chunks) * E_CHUNK, step):
+                cols = slice(lo, lo + step)
+                quantize(nc, h_codes[:, cols], h_scales[:, cols], h_bf[g][:, cols, :].rearrange("p n t -> p (n t)"))
             h_mx.append((h_codes, h_scales))
             if g == 0:
                 quantize(nc, w4_codes[:], w4_scales[:], w4_bf[:].rearrange("p c j -> p (c j)"))
 
         out_rows = out.rearrange("(a p) n -> p a n", p=P)
-        stores = ((0, 0, 1, True), (0, 1, 1, True), (1, 0, 2, False), (2, 0, 2, False))
+        stores = ((0, 0, 1, True), (0, 1, 1, True), (1, 0, 1, False), (1, 1, 1, True))
         for g, a0, blocks, on_scalar in stores:
             chunks = groups[g]
             width = len(chunks) * E_CHUNK

@@ -66,7 +66,8 @@ def tile_picked_edgeup_gelu_e_kernel(tc, xT, eT, w1, w2, w3, w4, offs, out):
         x_planes = []
         for j in range(PACK):
             plane = sb.tile([P, T], F32, name="x_plane%d" % j, align_bytes=64)
-            nc.sync.dma_start(out=plane[:], in_=x_rows[:, j, :])
+            for cols in (slice(0, T),) if j < PACK - 1 else (slice(0, T // 2), slice(T // 2, T)):
+                nc.sync.dma_start(out=plane[:, cols], in_=x_rows[:, j, cols])
             x_planes.append(plane)
             if j == 0:
                 nc.sync.dma_start(offsets[:], offs)
@@ -80,23 +81,25 @@ def tile_picked_edgeup_gelu_e_kernel(tc, xT, eT, w1, w2, w3, w4, offs, out):
         nc.scalar.activation(no_bias[:], zero[:], GELU)
 
         end_bf = [sb.tile([P, V, PACK], BF16, name="end_bf%d" % a, align_bytes=64) for a in range(2)]
-        first_pair = sb.tile([P, 2, S], BF16, name="first_pair", align_bytes=64)
-        nc.vector.tensor_copy(first_pair[:, 0, :], x_planes[0][:].indirect(offsets[:]))
-        plane1_bf = sb.tile([P, T], BF16, name="plane1_bf", align_bytes=64)
+        src_list, dst_list = offsets[:, 0 : V // 16], offsets[:, V // 16 : S // 16]
+        src = sb.tile([P, PACK, V], F32, name="src", align_bytes=64)
+        dst_pairs = [sb.tile([P, 2, V], BF16, name="dst_pair%d" % u, align_bytes=64) for u in range(2)]
+        for j in range(PACK - 1):
+            nc.vector.tensor_copy(dst_pairs[j // 2][:, j % 2, :], x_planes[j][:].indirect(dst_list))
+            nc.vector.tensor_copy(src[:, j, :], x_planes[j][:].indirect(src_list))
+            if j == 1:
+                weave_pair(nc, True, end_bf[1][:], 0, dst_pairs[0][:])
+        last_bf = sb.tile([P, T], BF16, name="last_bf", align_bytes=64)
+        for lo, hi, on_scalar in ((0, T // 2, True), (T // 2, 3 * T // 4, True), (3 * T // 4, T, False)):
+            cast(nc, on_scalar, last_bf[:, lo:hi], x_planes[3][:, lo:hi])
+        nc.scalar.activation(dst_pairs[1][:, 1, :], last_bf[:].indirect(dst_list), COPY)
         for half in range(2):
-            cols = slice(half * (T // 2), (half + 1) * (T // 2))
-            cast(nc, half == 0, plane1_bf[:, cols], x_planes[1][:, cols])
-        nc.scalar.activation(first_pair[:, 1, 0:V], plane1_bf[:].indirect(offsets[:, 0 : V // 16]), COPY)
-        nc.vector.tensor_copy(first_pair[:, 1, V:S], x_planes[1][:].indirect(offsets[:, V // 16 : S // 16]))
-        for a in range(2):
-            weave_pair(nc, True, end_bf[a][:], 0, first_pair[:, :, a * V : (a + 1) * V])
-        second_pair = [sb.tile([P, 2, V], F32, name="second_pair%d" % a, align_bytes=64) for a in range(2)]
-        for j in range(2):
-            for a in range(2):
-                piece = offsets[:, a * (V // 16) : (a + 1) * (V // 16)]
-                nc.vector.tensor_copy(second_pair[a][:, j, :], x_planes[2 + j][:].indirect(piece))
-        for a in range(2):
-            weave_pair(nc, False, end_bf[a][:], 1, second_pair[a][:])
+            cols = slice(half * (V // 2), (half + 1) * (V // 2))
+            nc.vector.tensor_copy(src[:, 3, cols], x_planes[3][:].indirect(offsets[:, cols.start // 16 : cols.stop // 16]))
+        for half in range(2):
+            cols = slice(half * (V // 2), (half + 1) * (V // 2))
+            weave(nc, False, end_bf[0][:, cols, :], src[:, :, cols])
+        weave_pair(nc, False, end_bf[1][:], 1, dst_pairs[1][:])
         ends = []
 
         def quantize_end(a, scales_tag):
@@ -121,23 +124,25 @@ def tile_picked_edgeup_gelu_e_kernel(tc, xT, eT, w1, w2, w3, w4, offs, out):
                     stop=(a == 2 and t == PACK - 1),
                 )
 
-        def cast_w(a, lo, tiles, on_scalar):
+        def cast_w(a, lo, tiles, vector_share):
             dealt = w_raw[a][:].rearrange("p j (m t) -> p m j t", t=PACK)
             part = sb.tile([P, tiles, P, PACK], BF16, name="w%d_bf%d" % (a, lo), align_bytes=64)
-            cast(nc, on_scalar, part[:].rearrange("p t m j -> p m j t"), dealt[:, :, :, lo : lo + tiles])
+            for m, on_scalar in ((slice(0, vector_share), False), (slice(vector_share, P), True)):
+                if m.stop > m.start:
+                    cast(nc, on_scalar, part[:, :, m, :].rearrange("p t m j -> p m j t"), dealt[:, m, :, lo : lo + tiles])
             return part
 
         def quantize_w(a, lo, tiles, part):
             cols = slice(lo * P, (lo + tiles) * P)
             quantize(nc, w_mx[a][0][:, cols], w_mx[a][1][:, cols], part[:].rearrange("p t m j -> p (t m j)"))
 
-        halves = [cast_w(0, lo, 2, True) for lo in (0, 2)]
+        halves = [cast_w(0, lo, 2, 0) for lo in (0, 2)]
         quantize_end(0, "end0_scales")
         quantize_w(0, 0, 2, halves[0])
         quantize_end(1, "w0_bf0")
         quantize_w(0, 2, 2, halves[1])
-        for a in (1, 2):
-            halves = [cast_w(a, lo, 2, a == 1 or lo == 2) for lo in (0, 2)]
+        for a, shares in ((1, (0, P // 2)), (2, (P, 0))):
+            halves = [cast_w(a, lo, 2, shares[lo // 2]) for lo in (0, 2)]
             for lo in (0, 2):
                 quantize_w(a, lo, 2, halves[lo // 2])
 

@@ -7,7 +7,6 @@ FLOPS = 2 * (3 * K * H * V + H * N * V)
 
 F32 = mybir.dt.float32
 BF16 = mybir.dt.bfloat16
-I32 = mybir.dt.int32
 U32 = mybir.dt.uint32
 U16 = mybir.dt.uint16
 U8 = mybir.dt.uint8
@@ -17,35 +16,41 @@ GELU = mybir.ActivationFunctionType.Gelu_apprx_tanh
 
 P = 128
 PACK = 4
-E_CHUNK = 128
+CHUNK = 128
+CHUNKS = V // CHUNK
 
 
-def cast(nc, on_scalar, dst, src):
+def move(nc, on_scalar, dst, src):
     if on_scalar:
         nc.scalar.activation(dst, src, COPY)
     else:
         nc.vector.tensor_copy(dst, src)
 
 
-def weave(nc, on_scalar, grouped, raw):
-    cast(nc, on_scalar, grouped.rearrange("p (c i) j -> p c j i", i=4), raw.rearrange("p j (c i) -> p c j i", i=4))
-
-
-def weave_dealt(nc, on_scalar, grouped, raw):
-    cast(nc, on_scalar, grouped.rearrange("p t m j -> p m j t"), raw.rearrange("p j (m t) -> p m j t", t=PACK))
+def weave(nc, on_scalar, grouped, rows, first=0):
+    count = rows.shape[1]
+    slots = grouped.rearrange("p (c i) j -> p c j i", i=4)[:, :, first : first + count, :]
+    move(nc, on_scalar, slots, rows.rearrange("p j (c i) -> p c j i", i=4))
 
 
 def quantize(nc, codes, scales, grouped):
     nc.vector.quantize_mx(out=codes.bitcast(FP8X4), scales=scales, in_=grouped)
 
 
-def weave_pair(nc, on_scalar, grouped, u, picked):
-    cast(nc, on_scalar, grouped.rearrange("p (c i) j -> p c j i", i=4)[:, :, 2 * u : 2 * u + 2, :], picked.rearrange("p j (c i) -> p c j i", i=4))
+def product(nc, out, lhs, rhs, start, stop):
+    nc.tensor.matmul_mx(
+        out=out,
+        lhsT=lhs[0].bitcast(FP8X4),
+        lhsT_scale=lhs[1],
+        rhs=rhs[0].bitcast(FP8X4),
+        rhs_scale=rhs[1],
+        start=start,
+        stop=stop,
+    )
 
 
 def tile_picked_edgeup_gelu_e_kernel(tc, xT, eT, w1, w2, w3, w4, offs, out):
     nc = tc.nc
-    e_chunks = V // E_CHUNK
 
     with ExitStack() as ctx:
         sb = ctx.enter_context(tc.tile_pool(name="sb", bufs=1))
@@ -61,13 +66,15 @@ def tile_picked_edgeup_gelu_e_kernel(tc, xT, eT, w1, w2, w3, w4, offs, out):
             scales = sb.tile([P, width], U8, name=name + "_scales", align_bytes=64)
             return codes, scales
 
+        def columns(mx, cols):
+            return mx[0][:, cols], mx[1][:, cols]
+
         x_rows = xT.rearrange("(p j) t -> p j t", j=PACK)
         offsets = sb.tile([P, S // 16], U16, name="offsets")
         x_planes = []
         for j in range(PACK):
             plane = sb.tile([P, T], F32, name="x_plane%d" % j, align_bytes=64)
-            for cols in (slice(0, T),) if j < PACK - 1 else (slice(0, T // 2), slice(T // 2, T)):
-                nc.sync.dma_start(out=plane[:, cols], in_=x_rows[:, j, cols])
+            nc.sync.dma_start(out=plane[:], in_=x_rows[:, j, :])
             x_planes.append(plane)
             if j == 0:
                 nc.sync.dma_start(offsets[:], offs)
@@ -81,130 +88,83 @@ def tile_picked_edgeup_gelu_e_kernel(tc, xT, eT, w1, w2, w3, w4, offs, out):
         nc.scalar.activation(no_bias[:], zero[:], GELU)
 
         end_bf = [sb.tile([P, V, PACK], BF16, name="end_bf%d" % a, align_bytes=64) for a in range(2)]
-        src_list, dst_list = offsets[:, 0 : V // 16], offsets[:, V // 16 : S // 16]
-        src = sb.tile([P, PACK, V], F32, name="src", align_bytes=64)
-        dst_pairs = [sb.tile([P, 2, V], BF16, name="dst_pair%d" % u, align_bytes=64) for u in range(2)]
+        picked = [[sb.tile([P, 2, V], BF16, name="picked%d_%d" % (a, u), align_bytes=64) for u in range(2)] for a in range(2)]
+        halves = [slice(b * (V // 2), (b + 1) * (V // 2)) for b in range(2)]
+
+        def gather(a, j, cols):
+            entries = offsets[:, (a * V + cols.start) // 16 : (a * V + cols.stop) // 16]
+            move(nc, a == 1, picked[a][j // 2][:, j % 2, cols], x_planes[j][:].indirect(entries))
+
         for j in range(PACK - 1):
-            nc.vector.tensor_copy(dst_pairs[j // 2][:, j % 2, :], x_planes[j][:].indirect(dst_list))
-            nc.vector.tensor_copy(src[:, j, :], x_planes[j][:].indirect(src_list))
-            if j == 1:
-                weave_pair(nc, True, end_bf[1][:], 0, dst_pairs[0][:])
-        last_bf = sb.tile([P, T], BF16, name="last_bf", align_bytes=64)
-        for lo, hi, on_scalar in ((0, T // 2, True), (T // 2, 3 * T // 4, True), (3 * T // 4, T, False)):
-            cast(nc, on_scalar, last_bf[:, lo:hi], x_planes[3][:, lo:hi])
-        nc.scalar.activation(dst_pairs[1][:, 1, :], last_bf[:].indirect(dst_list), COPY)
-        for half in range(2):
-            cols = slice(half * (V // 2), (half + 1) * (V // 2))
-            nc.vector.tensor_copy(src[:, 3, cols], x_planes[3][:].indirect(offsets[:, cols.start // 16 : cols.stop // 16]))
-        for half in range(2):
-            cols = slice(half * (V // 2), (half + 1) * (V // 2))
-            weave(nc, False, end_bf[0][:, cols, :], src[:, :, cols])
-        weave_pair(nc, False, end_bf[1][:], 1, dst_pairs[1][:])
-        ends = []
+            for a in range(2):
+                gather(a, j, slice(0, V))
+                if j == 1:
+                    weave(nc, a == 1, end_bf[a][:], picked[a][0][:])
+        for a in range(2):
+            for cols in halves:
+                gather(a, PACK - 1, cols)
+        for cols in halves:
+            weave(nc, False, end_bf[0][:, cols, :], picked[0][1][:, :, cols], first=2)
+        weave(nc, True, end_bf[1][:, halves[0], :], picked[1][1][:, :, halves[0]], first=2)
+        weave(nc, False, end_bf[1][:, halves[1], :], picked[1][1][:, :, halves[1]], first=2)
+        end_mx = [mx_tiles("end%d" % a, V) for a in range(2)]
+        for a in range(2):
+            quantize(nc, end_mx[a][0][:], end_mx[a][1][:], end_bf[a][:].rearrange("p c j -> p (c j)"))
 
-        def quantize_end(a, scales_tag):
-            codes = sb.tile([P, V], U32, name="end%d_codes" % a, align_bytes=64)
-            scales = sb.tile([P, V], U8, name="end%d_scales" % a, tag=scales_tag, align_bytes=64)
-            quantize(nc, codes[:], scales[:], end_bf[a][:].rearrange("p c j -> p (c j)"))
-            ends.append((codes, scales))
-
-        h_ps = [ps.tile([P, PACK, E_CHUNK], F32, name="h_ps%d" % c) for c in range(e_chunks)]
         w_mx = [mx_tiles("w%d" % a, H) for a in range(3)]
-
-        def first_layer_passes(a, c, codes, scales, tiles):
-            for t in tiles:
-                m = slice(t * P, (t + 1) * P)
-                nc.tensor.matmul_mx(
-                    out=h_ps[c][:, t, :],
-                    lhsT=w_mx[a][0][:, m].bitcast(FP8X4),
-                    lhsT_scale=w_mx[a][1][:, m],
-                    rhs=codes.bitcast(FP8X4),
-                    rhs_scale=scales,
-                    start=(a == 0 and t == 0),
-                    stop=(a == 2 and t == PACK - 1),
-                )
-
-        def cast_w(a, lo, tiles, vector_share):
+        for a in range(3):
             dealt = w_raw[a][:].rearrange("p j (m t) -> p m j t", t=PACK)
-            part = sb.tile([P, tiles, P, PACK], BF16, name="w%d_bf%d" % (a, lo), align_bytes=64)
-            for m, on_scalar in ((slice(0, vector_share), False), (slice(vector_share, P), True)):
-                if m.stop > m.start:
-                    cast(nc, on_scalar, part[:, :, m, :].rearrange("p t m j -> p m j t"), dealt[:, m, :, lo : lo + tiles])
-            return part
-
-        def quantize_w(a, lo, tiles, part):
-            cols = slice(lo * P, (lo + tiles) * P)
-            quantize(nc, w_mx[a][0][:, cols], w_mx[a][1][:, cols], part[:].rearrange("p t m j -> p (t m j)"))
-
-        halves = [cast_w(0, lo, 2, 0) for lo in (0, 2)]
-        quantize_end(0, "end0_scales")
-        quantize_w(0, 0, 2, halves[0])
-        quantize_end(1, "w0_bf0")
-        quantize_w(0, 2, 2, halves[1])
-        for a, shares in ((1, (0, P // 2)), (2, (P, 0))):
-            halves = [cast_w(a, lo, 2, shares[lo // 2]) for lo in (0, 2)]
+            parts = []
             for lo in (0, 2):
-                quantize_w(a, lo, 2, halves[lo // 2])
+                part = sb.tile([P, 2, P, PACK], BF16, name="w%d_bf%d" % (a, lo), align_bytes=64)
+                on_scalar = a == 0 or (lo == 0) == (a == 1)
+                move(nc, on_scalar, part[:].rearrange("p t m j -> p m j t"), dealt[:, :, :, lo : lo + 2])
+                parts.append(part)
+            for lo in (0, 2):
+                cols = slice(lo * P, (lo + 2) * P)
+                quantize(nc, w_mx[a][0][:, cols], w_mx[a][1][:, cols], parts[lo // 2][:].rearrange("p t m j -> p (t m j)"))
 
         e_mx = []
-        for c in range(e_chunks):
-            e_bf = sb.tile([P, E_CHUNK, PACK], BF16, name="e_bf%d" % c, align_bytes=64)
-            lo = (c % 2) * E_CHUNK
-            weave(nc, c < 2, e_bf[:], e_raw[c // 2][:, :, lo : lo + E_CHUNK])
-            e_codes, e_scales = mx_tiles("e%d" % c, E_CHUNK)
-            quantize(nc, e_codes[:], e_scales[:], e_bf[:].rearrange("p c j -> p (c j)"))
-            e_mx.append((e_codes[:], e_scales[:]))
+        for c in range(CHUNKS):
+            e_bf = sb.tile([P, CHUNK, PACK], BF16, name="e_bf%d" % c, align_bytes=64)
+            lo = (c % 2) * CHUNK
+            weave(nc, c < 2, e_bf[:], e_raw[c // 2][:, :, lo : lo + CHUNK])
+            e_mx.append(mx_tiles("e%d" % c, CHUNK))
+            quantize(nc, e_mx[c][0][:], e_mx[c][1][:], e_bf[:].rearrange("p c j -> p (c j)"))
 
-        def end_passes(a, c, tiles):
-            cols = slice(c * E_CHUNK, (c + 1) * E_CHUNK)
-            first_layer_passes(a, c, ends[a][0][:, cols], ends[a][1][:, cols], tiles)
+        h_ps = [ps.tile([P, PACK, CHUNK], F32, name="h_ps%d" % c) for c in range(CHUNKS)]
 
-        groups = ((0, 1), (2, 3))
-        h_bf = [sb.tile([P, len(g) * E_CHUNK, PACK], BF16, name="h_bf%d" % g[0], align_bytes=64) for g in groups]
+        def first_layer(a, c, moving, tiles):
+            for t in tiles:
+                stationary = columns(w_mx[a], slice(t * P, (t + 1) * P))
+                product(nc, h_ps[c][:, t, :], stationary, moving, a == 0 and t == 0, a == 2 and t == PACK - 1)
+
         for a in range(2):
             for tiles in ((0, 1), (2, 3)):
-                for c in range(e_chunks):
-                    end_passes(a, c, tiles)
-        for c in range(e_chunks):
-            first_layer_passes(2, c, e_mx[c][0], e_mx[c][1], range(PACK))
-        for g, chunks in enumerate(groups):
-            for c in chunks:
-                cols = slice((c - chunks[0]) * E_CHUNK, (c - chunks[0] + 1) * E_CHUNK)
-                nc.scalar.activation(h_bf[g][:, cols, :], h_ps[c][:].rearrange("p t n -> p n t"), GELU, bias=no_bias[:])
+                for c in range(CHUNKS):
+                    first_layer(a, c, columns(end_mx[a], slice(c * CHUNK, (c + 1) * CHUNK)), tiles)
+        for c in range(CHUNKS):
+            first_layer(2, c, columns(e_mx[c], slice(0, CHUNK)), range(PACK))
+        h_bf = [sb.tile([P, V // 2, PACK], BF16, name="h_bf%d" % b, align_bytes=64) for b in range(2)]
+        for c in range(CHUNKS):
+            cols = slice((c % 2) * CHUNK, (c % 2 + 1) * CHUNK)
+            nc.scalar.activation(h_bf[c // 2][:, cols, :], h_ps[c][:].rearrange("p t n -> p n t"), GELU, bias=no_bias[:])
 
         w4_bf = sb.tile([P, N, PACK], BF16, name="w4_bf", align_bytes=64)
         weave(nc, False, w4_bf[:], w4_raw[:])
-        w4_codes, w4_scales = mx_tiles("w4", N)
-        h_mx = []
-        for g, chunks in enumerate(groups):
-            h_codes, h_scales = mx_tiles("h%d" % g, len(chunks) * E_CHUNK)
-            step = len(chunks) * E_CHUNK if g == 0 else E_CHUNK
-            for lo in range(0, len(chunks) * E_CHUNK, step):
-                cols = slice(lo, lo + step)
-                quantize(nc, h_codes[:, cols], h_scales[:, cols], h_bf[g][:, cols, :].rearrange("p n t -> p (n t)"))
-            h_mx.append((h_codes, h_scales))
-            if g == 0:
-                quantize(nc, w4_codes[:], w4_scales[:], w4_bf[:].rearrange("p c j -> p (c j)"))
+        w4_mx = mx_tiles("w4", N)
+        h_mx = [mx_tiles("h%d" % b, V // 2) for b in range(2)]
+        quantize(nc, h_mx[0][0][:], h_mx[0][1][:], h_bf[0][:].rearrange("p n t -> p (n t)"))
+        quantize(nc, w4_mx[0][:], w4_mx[1][:], w4_bf[:].rearrange("p c j -> p (c j)"))
+        for lo in (0, CHUNK):
+            cols = slice(lo, lo + CHUNK)
+            quantize(nc, h_mx[1][0][:, cols], h_mx[1][1][:, cols], h_bf[1][:, cols, :].rearrange("p n t -> p (n t)"))
 
         out_rows = out.rearrange("(a p) n -> p a n", p=P)
-        stores = ((0, 0, 1, True), (0, 1, 1, True), (1, 0, 1, False), (1, 1, 1, True))
-        for g, a0, blocks, on_scalar in stores:
-            chunks = groups[g]
-            width = len(chunks) * E_CHUNK
-            h_codes, h_scales = h_mx[g]
-            o_ps = ps.tile([P, blocks, width], F32, name="o_ps%d_%d" % (g, a0))
-            for a in range(blocks):
-                m = slice((a0 + a) * P, (a0 + a + 1) * P)
-                nc.tensor.matmul_mx(
-                    out=o_ps[:, a, :],
-                    lhsT=w4_codes[:, m].bitcast(FP8X4),
-                    lhsT_scale=w4_scales[:, m],
-                    rhs=h_codes[:].bitcast(FP8X4),
-                    rhs_scale=h_scales[:],
-                    start=True,
-                    stop=True,
-                )
-            o_sb = sb.tile([P, blocks, width], F32, name="o_sb%d_%d" % (g, a0), align_bytes=64)
-            cast(nc, on_scalar, o_sb[:], o_ps[:])
-            lo = chunks[0] * E_CHUNK
-            nc.sync.dma_start(out=out_rows[:, a0 : a0 + blocks, lo : lo + width], in_=o_sb[:])
+        for b in range(2):
+            for a in range(N // P):
+                o_ps = ps.tile([P, V // 2], F32, name="o_ps%d_%d" % (b, a))
+                product(nc, o_ps[:], columns(w4_mx, slice(a * P, (a + 1) * P)), columns(h_mx[b], slice(0, V // 2)), True, True)
+                o_sb = sb.tile([P, V // 2], F32, name="o_sb%d_%d" % (b, a), align_bytes=64)
+                move(nc, (b, a) != (1, 0), o_sb[:], o_ps[:])
+                nc.sync.dma_start(out=out_rows[:, a, halves[b]], in_=o_sb[:])

@@ -18,6 +18,8 @@ P = 128
 PACK = 4
 CHUNK = 128
 CHUNKS = V // CHUNK
+SCALAR_SHARE = ((P, P), (P, 0), (0, 3 * P // 4))
+E_SCALAR_SHARE = (CHUNK // 2, CHUNK, 0, 0)
 
 
 def move(nc, on_scalar, dst, src):
@@ -117,8 +119,10 @@ def tile_picked_edgeup_gelu_e_kernel(tc, xT, eT, w1, w2, w3, w4, offs, out):
             parts = []
             for lo in (0, 2):
                 part = sb.tile([P, 2, P, PACK], BF16, name="w%d_bf%d" % (a, lo), align_bytes=64)
-                on_scalar = a == 0 or (lo == 0) == (a == 1)
-                move(nc, on_scalar, part[:].rearrange("p t m j -> p m j t"), dealt[:, :, :, lo : lo + 2])
+                split = SCALAR_SHARE[a][lo // 2]
+                for m, on_scalar in ((slice(0, split), True), (slice(split, P), False)):
+                    if m.stop > m.start:
+                        move(nc, on_scalar, part[:, :, m, :].rearrange("p t m j -> p m j t"), dealt[:, m, :, lo : lo + 2])
                 parts.append(part)
             for lo in (0, 2):
                 cols = slice(lo * P, (lo + 2) * P)
@@ -128,11 +132,14 @@ def tile_picked_edgeup_gelu_e_kernel(tc, xT, eT, w1, w2, w3, w4, offs, out):
         for c in range(CHUNKS):
             e_bf = sb.tile([P, CHUNK, PACK], BF16, name="e_bf%d" % c, align_bytes=64)
             lo = (c % 2) * CHUNK
-            weave(nc, c < 2, e_bf[:], e_raw[c // 2][:, :, lo : lo + CHUNK])
+            split = E_SCALAR_SHARE[c]
+            for n, on_scalar in ((slice(0, split), True), (slice(split, CHUNK), False)):
+                if n.stop > n.start:
+                    weave(nc, on_scalar, e_bf[:, n, :], e_raw[c // 2][:, :, lo + n.start : lo + n.stop])
             e_mx.append(mx_tiles("e%d" % c, CHUNK))
             quantize(nc, e_mx[c][0][:], e_mx[c][1][:], e_bf[:].rearrange("p c j -> p (c j)"))
 
-        h_ps = [ps.tile([P, PACK, CHUNK], F32, name="h_ps%d" % c) for c in range(CHUNKS)]
+        h_ps = [ps.tile([P, PACK, CHUNK], F32, name="h_ps%d" % c, tag="h_ps%d" % c) for c in range(CHUNKS)]
 
         def first_layer(a, c, moving, tiles):
             for t in tiles:
@@ -150,21 +157,36 @@ def tile_picked_edgeup_gelu_e_kernel(tc, xT, eT, w1, w2, w3, w4, offs, out):
             cols = slice((c % 2) * CHUNK, (c % 2 + 1) * CHUNK)
             nc.scalar.activation(h_bf[c // 2][:, cols, :], h_ps[c][:].rearrange("p t n -> p n t"), GELU, bias=no_bias[:])
 
-        w4_bf = sb.tile([P, N, PACK], BF16, name="w4_bf", align_bytes=64)
-        weave(nc, False, w4_bf[:], w4_raw[:])
         w4_mx = mx_tiles("w4", N)
         h_mx = [mx_tiles("h%d" % b, V // 2) for b in range(2)]
+        w4_bf = [sb.tile([P, P, PACK], BF16, name="w4_bf%d" % a, align_bytes=64) for a in range(N // P)]
+        for a in range(N // P):
+            weave(nc, False, w4_bf[a][:], w4_raw[:, :, a * P : (a + 1) * P])
         quantize(nc, h_mx[0][0][:], h_mx[0][1][:], h_bf[0][:].rearrange("p n t -> p (n t)"))
-        quantize(nc, w4_mx[0][:], w4_mx[1][:], w4_bf[:].rearrange("p c j -> p (c j)"))
+        for a in range(N // P):
+            cols = slice(a * P, (a + 1) * P)
+            quantize(nc, w4_mx[0][:, cols], w4_mx[1][:, cols], w4_bf[a][:].rearrange("p c j -> p (c j)"))
         for lo in (0, CHUNK):
             cols = slice(lo, lo + CHUNK)
             quantize(nc, h_mx[1][0][:, cols], h_mx[1][1][:, cols], h_bf[1][:, cols, :].rearrange("p n t -> p (n t)"))
 
         out_rows = out.rearrange("(a p) n -> p a n", p=P)
-        for b in range(2):
-            for a in range(N // P):
-                o_ps = ps.tile([P, V // 2], F32, name="o_ps%d_%d" % (b, a))
-                product(nc, o_ps[:], columns(w4_mx, slice(a * P, (a + 1) * P)), columns(h_mx[b], slice(0, V // 2)), True, True)
-                o_sb = sb.tile([P, V // 2], F32, name="o_sb%d_%d" % (b, a), align_bytes=64)
-                move(nc, (b, a) != (1, 0), o_sb[:], o_ps[:])
-                nc.sync.dma_start(out=out_rows[:, a, halves[b]], in_=o_sb[:])
+        w4_halves = [columns(w4_mx, slice(a * P, (a + 1) * P)) for a in range(N // P)]
+        for a in range(N // P):
+            first_ps = ps.tile([P, V // 2], F32, name="first_ps%d" % a)
+            product(nc, first_ps[:], w4_halves[a], columns(h_mx[0], slice(0, V // 2)), True, True)
+            o_sb = sb.tile([P, V // 2], F32, name="first_sb%d" % a, align_bytes=64)
+            move(nc, True, o_sb[:], first_ps[:])
+            nc.sync.dma_start(out=out_rows[:, a, halves[0]], in_=o_sb[:])
+        third_ps = ps.tile([P, N // P, CHUNK], F32, name="third_ps")
+        for a in range(N // P):
+            product(nc, third_ps[:, a, :], w4_halves[a], columns(h_mx[1], slice(0, CHUNK)), True, True)
+        third_sb = sb.tile([P, N // P, CHUNK], F32, name="third_sb", align_bytes=64)
+        move(nc, False, third_sb[:], third_ps[:])
+        nc.sync.dma_start(out=out_rows[:, :, 2 * CHUNK : 3 * CHUNK], in_=third_sb[:])
+        last_sb = sb.tile([P, N // P, CHUNK], F32, name="last_sb", align_bytes=64)
+        for a in range(N // P):
+            last_ps = ps.tile([P, CHUNK], F32, name="last_ps%d" % a, tag="h_ps%d" % a)
+            product(nc, last_ps[:], w4_halves[a], columns(h_mx[1], slice(CHUNK, 2 * CHUNK)), True, True)
+            move(nc, a == 1, last_sb[:, a, :], last_ps[:])
+        nc.sync.dma_start(out=out_rows[:, :, 3 * CHUNK : V], in_=last_sb[:])

@@ -18,8 +18,8 @@ P = 128
 PACK = 4
 CHUNK = 128
 CHUNKS = V // CHUNK
-SCALAR_SHARE = ((P, P), (P, 0), (0, 3 * P // 4))
-E_SCALAR_SHARE = (CHUNK // 2, CHUNK, 0, 0)
+SCALAR_SHARE = ((P, P), (P, 0), (0, P))
+E_SCALAR_SHARE = (0, CHUNK, 0, 0)
 
 
 def move(nc, on_scalar, dst, src):
@@ -178,15 +178,13 @@ def tile_picked_edgeup_gelu_e_kernel(tc, xT, eT, w1, w2, w3, w4, offs, out):
             o_sb = sb.tile([P, V // 2], F32, name="first_sb%d" % a, align_bytes=64)
             move(nc, True, o_sb[:], first_ps[:])
             nc.sync.dma_start(out=out_rows[:, a, halves[0]], in_=o_sb[:])
+        second_sb = sb.tile([P, N // P, V // 2], F32, name="second_sb", align_bytes=64)
         third_ps = ps.tile([P, N // P, CHUNK], F32, name="third_ps")
         for a in range(N // P):
             product(nc, third_ps[:, a, :], w4_halves[a], columns(h_mx[1], slice(0, CHUNK)), True, True)
-        third_sb = sb.tile([P, N // P, CHUNK], F32, name="third_sb", align_bytes=64)
-        move(nc, False, third_sb[:], third_ps[:])
-        nc.sync.dma_start(out=out_rows[:, :, 2 * CHUNK : 3 * CHUNK], in_=third_sb[:])
-        last_sb = sb.tile([P, N // P, CHUNK], F32, name="last_sb", align_bytes=64)
+        move(nc, False, second_sb[:, :, 0:CHUNK], third_ps[:])
         for a in range(N // P):
             last_ps = ps.tile([P, CHUNK], F32, name="last_ps%d" % a, tag="h_ps%d" % a)
             product(nc, last_ps[:], w4_halves[a], columns(h_mx[1], slice(CHUNK, 2 * CHUNK)), True, True)
-            move(nc, a == 1, last_sb[:, a, :], last_ps[:])
-        nc.sync.dma_start(out=out_rows[:, :, 3 * CHUNK : V], in_=last_sb[:])
+            move(nc, a == 1, second_sb[:, a, CHUNK : 2 * CHUNK], last_ps[:])
+        nc.sync.dma_start(out=out_rows[:, :, halves[1]], in_=second_sb[:])

@@ -18,7 +18,7 @@ P = 128
 PACK = 4
 CHUNK = 128
 CHUNKS = V // CHUNK
-SCALAR_SHARE = ((P, P), (P, 0), (0, P))
+SCALAR_SHARE = ((P, P), (P // 2, 0), (0, P))
 E_SCALAR_SHARE = (0, CHUNK, 0, 0)
 
 
@@ -90,25 +90,24 @@ def tile_picked_edgeup_gelu_e_kernel(tc, xT, eT, w1, w2, w3, w4, offs, out):
         nc.scalar.activation(no_bias[:], zero[:], GELU)
 
         end_bf = [sb.tile([P, V, PACK], BF16, name="end_bf%d" % a, align_bytes=64) for a in range(2)]
-        picked = [[sb.tile([P, 2, V], BF16, name="picked%d_%d" % (a, u), align_bytes=64) for u in range(2)] for a in range(2)]
+        src_rows = sb.tile([P, PACK - 1, V], BF16, name="src_rows", align_bytes=64)
+        dst_pairs = [sb.tile([P, 2, V], BF16, name="dst_pair%d" % u, align_bytes=64) for u in range(2)]
         halves = [slice(b * (V // 2), (b + 1) * (V // 2)) for b in range(2)]
 
-        def gather(a, j, cols):
-            entries = offsets[:, (a * V + cols.start) // 16 : (a * V + cols.stop) // 16]
-            move(nc, a == 1, picked[a][j // 2][:, j % 2, cols], x_planes[j][:].indirect(entries))
+        def picked(a, j, cols):
+            return x_planes[j][:].indirect(offsets[:, (a * V + cols.start) // 16 : (a * V + cols.stop) // 16])
 
         for j in range(PACK - 1):
-            for a in range(2):
-                gather(a, j, slice(0, V))
-                if j == 1:
-                    weave(nc, a == 1, end_bf[a][:], picked[a][0][:])
-        for a in range(2):
-            for cols in halves:
-                gather(a, PACK - 1, cols)
+            move(nc, False, src_rows[:, j, :], picked(0, j, slice(0, V)))
+            move(nc, True, dst_pairs[j // 2][:, j % 2, :], picked(1, j, slice(0, V)))
+            if j == 1:
+                weave(nc, True, end_bf[1][:], dst_pairs[0][:])
+        weave(nc, False, end_bf[0][:], src_rows[:])
+        move(nc, False, end_bf[0][:, :, PACK - 1], picked(0, PACK - 1, slice(0, V)))
         for cols in halves:
-            weave(nc, False, end_bf[0][:, cols, :], picked[0][1][:, :, cols], first=2)
-        weave(nc, True, end_bf[1][:, halves[0], :], picked[1][1][:, :, halves[0]], first=2)
-        weave(nc, False, end_bf[1][:, halves[1], :], picked[1][1][:, :, halves[1]], first=2)
+            move(nc, True, dst_pairs[1][:, 1, cols], picked(1, PACK - 1, cols))
+        weave(nc, True, end_bf[1][:, halves[0], :], dst_pairs[1][:, :, halves[0]], first=2)
+        weave(nc, False, end_bf[1][:, halves[1], :], dst_pairs[1][:, :, halves[1]], first=2)
         end_mx = [mx_tiles("end%d" % a, V) for a in range(2)]
         for a in range(2):
             quantize(nc, end_mx[a][0][:], end_mx[a][1][:], end_bf[a][:].rearrange("p c j -> p (c j)"))

from contextlib import ExitStack

import concourse.mybir as mybir

K, T, S, V, H, N = 512, 2048, 1024, 512, 512, 256
FLOPS = 2 * (3 * K * H * V + H * N * V)

F32 = mybir.dt.float32
BF16 = mybir.dt.bfloat16
U32 = mybir.dt.uint32
U16 = mybir.dt.uint16
U8 = mybir.dt.uint8
FP8X4 = mybir.dt.float8_e4m3fn_x4
COPY = mybir.ActivationFunctionType.Copy
GELU = mybir.ActivationFunctionType.Gelu_apprx_tanh

P = 128
PACK = 4
CHUNK = 128
CHUNKS = V // CHUNK
SCALAR_SHARE = ((P, P), (P // 2, 0), (0, P))
E_SCALAR_SHARE = (0, CHUNK, 0, 0)


def move(nc, on_scalar, dst, src):
    if on_scalar:
        nc.scalar.activation(dst, src, COPY)
    else:
        nc.vector.tensor_copy(dst, src)


def weave(nc, on_scalar, grouped, rows, first=0):
    count = rows.shape[1]
    slots = grouped.rearrange("p (c i) j -> p c j i", i=4)[:, :, first : first + count, :]
    move(nc, on_scalar, slots, rows.rearrange("p j (c i) -> p c j i", i=4))


def quantize(nc, codes, scales, grouped):
    nc.vector.quantize_mx(out=codes.bitcast(FP8X4), scales=scales, in_=grouped)


def product(nc, out, lhs, rhs, start, stop):
    nc.tensor.matmul_mx(
        out=out,
        lhsT=lhs[0].bitcast(FP8X4),
        lhsT_scale=lhs[1],
        rhs=rhs[0].bitcast(FP8X4),
        rhs_scale=rhs[1],
        start=start,
        stop=stop,
    )


def tile_picked_edgeup_gelu_e_kernel(tc, xT, eT, w1, w2, w3, w4, offs, out):
    nc = tc.nc

    with ExitStack() as ctx:
        sb = ctx.enter_context(tc.tile_pool(name="sb", bufs=1))
        ps = ctx.enter_context(tc.psum_pool(name="ps", bufs=1))

        def load(name, rows):
            raw = sb.tile([P, PACK, rows.shape[1]], F32, name=name, align_bytes=64)
            nc.sync.dma_start(out=raw[:], in_=rows.rearrange("(p j) w -> p j w", j=PACK))
            return raw

        def mx_tiles(name, width):
            codes = sb.tile([P, width], U32, name=name + "_codes", align_bytes=64)
            scales = sb.tile([P, width], U8, name=name + "_scales", align_bytes=64)
            return codes, scales

        def columns(mx, cols):
            return mx[0][:, cols], mx[1][:, cols]

        x_rows = xT.rearrange("(p j) t -> p j t", j=PACK)
        offsets = sb.tile([P, S // 16], U16, name="offsets")
        x_planes = []
        for j in range(PACK):
            plane = sb.tile([P, T], F32, name="x_plane%d" % j, align_bytes=64)
            nc.sync.dma_start(out=plane[:], in_=x_rows[:, j, :])
            x_planes.append(plane)
            if j == 0:
                nc.sync.dma_start(offsets[:], offs)
        w_raw = [load("w_raw%d" % a, w) for a, w in enumerate((w1, w2, w3))]
        e_raw = [load("e_raw%d" % b, eT[:, b * (V // 2) : (b + 1) * (V // 2)]) for b in range(2)]
        w4_raw = load("w4_raw", w4)

        zero = sb.tile([P, 1], F32, name="zero")
        no_bias = sb.tile([P, 1], F32, name="no_bias")
        nc.vector.memset(zero[:], 0.0)
        nc.scalar.activation(no_bias[:], zero[:], GELU)

        end_bf = [sb.tile([P, V, PACK], BF16, name="end_bf%d" % a, align_bytes=64) for a in range(2)]
        src_rows = sb.tile([P, PACK - 1, V], BF16, name="src_rows", align_bytes=64)
        dst_pairs = [sb.tile([P, 2, V], BF16, name="dst_pair%d" % u, align_bytes=64) for u in range(2)]
        halves = [slice(b * (V // 2), (b + 1) * (V // 2)) for b in range(2)]

        def picked(a, j, cols):
            return x_planes[j][:].indirect(offsets[:, (a * V + cols.start) // 16 : (a * V + cols.stop) // 16])

        for j in range(PACK - 1):
            move(nc, False, src_rows[:, j, :], picked(0, j, slice(0, V)))
            move(nc, True, dst_pairs[j // 2][:, j % 2, :], picked(1, j, slice(0, V)))
            if j == 1:
                weave(nc, True, end_bf[1][:], dst_pairs[0][:])
        weave(nc, False, end_bf[0][:], src_rows[:])
        move(nc, False, end_bf[0][:, :, PACK - 1], picked(0, PACK - 1, slice(0, V)))
        for cols in halves:
            move(nc, True, dst_pairs[1][:, 1, cols], picked(1, PACK - 1, cols))
        weave(nc, True, end_bf[1][:, halves[0], :], dst_pairs[1][:, :, halves[0]], first=2)
        weave(nc, False, end_bf[1][:, halves[1], :], dst_pairs[1][:, :, halves[1]], first=2)
        end_mx = [mx_tiles("end%d" % a, V) for a in range(2)]
        for a in range(2):
            quantize(nc, end_mx[a][0][:], end_mx[a][1][:], end_bf[a][:].rearrange("p c j -> p (c j)"))

        w_mx = [mx_tiles("w%d" % a, H) for a in range(3)]
        for a in range(3):
            dealt = w_raw[a][:].rearrange("p j (m t) -> p m j t", t=PACK)
            parts = []
            for lo in (0, 2):
                part = sb.tile([P, 2, P, PACK], BF16, name="w%d_bf%d" % (a, lo), align_bytes=64)
                split = SCALAR_SHARE[a][lo // 2]
                for m, on_scalar in ((slice(0, split), True), (slice(split, P), False)):
                    if m.stop > m.start:
                        move(nc, on_scalar, part[:, :, m, :].rearrange("p t m j -> p m j t"), dealt[:, m, :, lo : lo + 2])
                parts.append(part)
            for lo in (0, 2):
                cols = slice(lo * P, (lo + 2) * P)
                quantize(nc, w_mx[a][0][:, cols], w_mx[a][1][:, cols], parts[lo // 2][:].rearrange("p t m j -> p (t m j)"))

        e_mx = []
        for c in range(CHUNKS):
            e_bf = sb.tile([P, CHUNK, PACK], BF16, name="e_bf%d" % c, align_bytes=64)
            lo = (c % 2) * CHUNK
            split = E_SCALAR_SHARE[c]
            for n, on_scalar in ((slice(0, split), True), (slice(split, CHUNK), False)):
                if n.stop > n.start:
                    weave(nc, on_scalar, e_bf[:, n, :], e_raw[c // 2][:, :, lo + n.start : lo + n.stop])
            e_mx.append(mx_tiles("e%d" % c, CHUNK))
            quantize(nc, e_mx[c][0][:], e_mx[c][1][:], e_bf[:].rearrange("p c j -> p (c j)"))

        h_ps = [ps.tile([P, PACK, CHUNK], F32, name="h_ps%d" % c, tag="h_ps%d" % c) for c in range(CHUNKS)]

        def first_layer(a, c, moving, tiles):
            for t in tiles:
                stationary = columns(w_mx[a], slice(t * P, (t + 1) * P))
                product(nc, h_ps[c][:, t, :], stationary, moving, a == 0 and t == 0, a == 2 and t == PACK - 1)

        for a in range(2):
            for tiles in ((0, 1), (2, 3)):
                for c in range(CHUNKS):
                    first_layer(a, c, columns(end_mx[a], slice(c * CHUNK, (c + 1) * CHUNK)), tiles)
        for c in range(CHUNKS):
            first_layer(2, c, columns(e_mx[c], slice(0, CHUNK)), range(PACK))
        h_bf = [sb.tile([P, V // 2, PACK], BF16, name="h_bf%d" % b, align_bytes=64) for b in range(2)]
        for c in range(CHUNKS):
            cols = slice((c % 2) * CHUNK, (c % 2 + 1) * CHUNK)
            nc.scalar.activation(h_bf[c // 2][:, cols, :], h_ps[c][:].rearrange("p t n -> p n t"), GELU, bias=no_bias[:])

        w4_mx = mx_tiles("w4", N)
        h_mx = [mx_tiles("h%d" % b, V // 2) for b in range(2)]
        w4_bf = [sb.tile([P, P, PACK], BF16, name="w4_bf%d" % a, align_bytes=64) for a in range(N // P)]
        for a in range(N // P):
            weave(nc, False, w4_bf[a][:], w4_raw[:, :, a * P : (a + 1) * P])
        quantize(nc, h_mx[0][0][:], h_mx[0][1][:], h_bf[0][:].rearrange("p n t -> p (n t)"))
        for a in range(N // P):
            cols = slice(a * P, (a + 1) * P)
            quantize(nc, w4_mx[0][:, cols], w4_mx[1][:, cols], w4_bf[a][:].rearrange("p c j -> p (c j)"))
        for lo in (0, CHUNK):
            cols = slice(lo, lo + CHUNK)
            quantize(nc, h_mx[1][0][:, cols], h_mx[1][1][:, cols], h_bf[1][:, cols, :].rearrange("p n t -> p (n t)"))

        out_rows = out.rearrange("(a p) n -> p a n", p=P)
        w4_halves = [columns(w4_mx, slice(a * P, (a + 1) * P)) for a in range(N // P)]
        for a in range(N // P):
            first_ps = ps.tile([P, V // 2], F32, name="first_ps%d" % a)
            product(nc, first_ps[:], w4_halves[a], columns(h_mx[0], slice(0, V // 2)), True, True)
            o_sb = sb.tile([P, V // 2], F32, name="first_sb%d" % a, align_bytes=64)
            move(nc, True, o_sb[:], first_ps[:])
            nc.sync.dma_start(out=out_rows[:, a, halves[0]], in_=o_sb[:])
        second_sb = sb.tile([P, N // P, V // 2], F32, name="second_sb", align_bytes=64)
        third_ps = ps.tile([P, N // P, CHUNK], F32, name="third_ps")
        for a in range(N // P):
            product(nc, third_ps[:, a, :], w4_halves[a], columns(h_mx[1], slice(0, CHUNK)), True, True)
        move(nc, False, second_sb[:, :, 0:CHUNK], third_ps[:])
        for a in range(N // P):
            last_ps = ps.tile([P, CHUNK], F32, name="last_ps%d" % a, tag="h_ps%d" % a)
            product(nc, last_ps[:], w4_halves[a], columns(h_mx[1], slice(CHUNK, 2 * CHUNK)), True, True)
            move(nc, a == 1, second_sb[:, a, CHUNK : 2 * CHUNK], last_ps[:])
        nc.sync.dma_start(out=out_rows[:, :, halves[1]], in_=second_sb[:])
